import numpy as np
import ml_dtypes


def mxq(x, axis, fmt="e4m3"):
    dtype, down = {"e4m3": (ml_dtypes.float8_e4m3fn, 7), "e5m2": (ml_dtypes.float8_e5m2, 14)}[fmt]
    v = np.moveaxis(np.asarray(x, np.float32).astype(ml_dtypes.bfloat16).astype(np.float64), axis, -1)
    blocks = v.reshape(v.shape[:-1] + (-1, 32))
    amax = np.abs(blocks).max(-1, keepdims=True)
    byte = np.maximum(np.where(amax > 0, np.frexp(amax)[1] - 1 + 127, 0) - down, 1)
    scale = np.exp2(byte - 127.0)
    codes = (blocks / scale).astype(np.float32).astype(dtype).astype(np.float64)
    return np.moveaxis((codes * scale).reshape(v.shape), -1, axis)


WIDE = False


def mx_kscale(k):
    if not WIDE:
        return np.ones(k)
    levels = np.array([30, -30])
    if k % 512:
        return np.exp2(np.random.permutation(np.resize(levels, k // 32))).repeat(32)
    a = np.empty((k // 512, 16))
    for p in range(k // 512):
        a[p, :8] = np.random.permutation(np.resize(levels, 8))
        for g in range(8):
            far = levels[np.abs(levels - a[p, g]) >= 10]
            a[p, g + 8] = far[np.random.randint(len(far))]
    return np.exp2(a.ravel()).repeat(32)


def f64(x):
    return np.asarray(x).astype(np.float64)


def striped(idx):
    return np.tile(np.asarray(idx).reshape(-1, 16).T, (8, 1)).astype(np.uint16)


def unstriped(offs):
    return offs[:16].T.reshape(-1).astype(np.int64)


E2M1 = np.array([0.0, 0.5, 1.0, 1.5, 2.0, 3.0, 4.0, 6.0, -0.0, -0.5, -1.0, -1.5, -2.0, -3.0, -4.0, -6.0])


def pack_weight(w, fmt):
    k, n = w.shape
    w = f64(np.asarray(w, np.float32).astype(ml_dtypes.bfloat16)).reshape(k // 32, 32, n)
    amax = np.abs(w).max(1)
    if fmt in ("e4m3", "e5m2"):
        byte = np.frexp(amax)[1] - 1 + 127 - (7 if fmt == "e4m3" else 14)
    else:
        mant, ex = np.frexp(amax / 6.0)
        byte = np.where(mant > 0.5, ex, ex - 1) + 127
    byte = np.clip(np.where(amax > 0, byte, 1), 1, 254)
    scaled = (w * np.exp2(127.0 - byte)[:, None, :]).reshape(k, n).astype(np.float32)
    by_word = np.ascontiguousarray(scaled.reshape(k // 512, 128, 4, n).transpose(0, 1, 3, 2))
    if fmt in ("e4m3", "e5m2"):
        words = by_word.astype(ml_dtypes.float8_e4m3fn if fmt == "e4m3" else ml_dtypes.float8_e5m2).view(np.uint8)
    else:
        c = by_word.astype(ml_dtypes.float4_e2m1fn).view(np.uint8) & 0xF
        words = (c[..., 0::2] | (c[..., 1::2] << 4)).reshape(k // 512, 128, 2 * n)
    return np.ascontiguousarray(words), np.ascontiguousarray(byte.astype(np.uint8).reshape(k // 512, 16, n))


def unpack_weight(words, scales, fmt):
    g, _, n = scales.shape
    words = np.ascontiguousarray(words).reshape(g, 128, n, -1)
    if fmt in ("e4m3", "e5m2"):
        vals = words.view(ml_dtypes.float8_e4m3fn if fmt == "e4m3" else ml_dtypes.float8_e5m2).astype(np.float64)
    else:
        nib = np.empty((g, 128, n, 4), np.uint8)
        nib[..., 0::2] = words & 0xF
        nib[..., 1::2] = words >> 4
        vals = E2M1[nib]
    vals = vals * np.repeat(np.exp2(scales.astype(np.float64) - 127.0), 8, axis=1)[..., None]
    return vals.transpose(0, 1, 3, 2).reshape(g * 512, n)


K, T, J, R, F, V, N = 512, 512, 256, 512, 512, 512, 256


def setup_inputs():
    n = np.random.standard_normal
    idx = np.random.permutation(T)[:J]
    idx2 = np.random.permutation(V)[:J]
    fk = mx_kscale(K)
    fr = mx_kscale(R)
    ff = mx_kscale(F)
    wp = pack_weight(n((K, R)) * 1 / np.sqrt(K) * fk[:, None] * fr, "e2m1")
    sxp = pack_weight(n((F, J)) / ff[:, None], "e4m3")
    w2p = pack_weight(n((F, R)) * 1 / np.sqrt(F) * ff[:, None] * fr, "e5m2")
    wbp = pack_weight(n((R, N)) * 1 / np.sqrt(R) / fr[:, None], "e5m2")
    return {
        "xf": (n((K, T))).astype(np.float32),
        "fk": (np.random.uniform(0.5, 2.0, (K, 1)) / fk[:, None]).astype(np.float32),
        "w_words": wp[0],
        "w_scales": wp[1],
        "sx_words": sxp[0],
        "sx_scales": sxp[1],
        "w2_words": w2p[0],
        "w2_scales": w2p[1],
        "tb": (n((R, V)) * 0.7 * fr[:, None]).astype(np.float32),
        "wb_words": wbp[0],
        "wb_scales": wbp[1],
        "rs": (n((N, J))).astype(np.float32),
        "offs": striped(idx),
        "offs2": striped(idx2),
    }


def reference(xf, fk, w_words, w_scales, sx_words, sx_scales, w2_words, w2_scales, tb, wb_words, wb_scales, rs, offs, offs2):
    idx = unstriped(offs)
    idx2 = unstriped(offs2)
    wu = unpack_weight(w_words, w_scales, "e2m1")
    sxu = unpack_weight(sx_words, sx_scales, "e4m3")
    w2u = unpack_weight(w2_words, w2_scales, "e5m2")
    wbu = unpack_weight(wb_words, wb_scales, "e5m2")
    xg = f64(xf)[:, idx]
    x1 = np.pad(xg, ((0, 0), (1, 0)))[:, :J]
    u = (xg - 0.6 * x1) * f64(fk)
    uq = mxq(u, 0, "e4m3")
    a = wu.T @ uq + w2u.T @ sxu
    hid = np.maximum(a - f64(tb)[:, idx2], 0.0)
    hidq = mxq(hid, 0, "e5m2")
    p = wbu.T @ hidq
    p1 = np.pad(p, ((0, 0), (1, 0)))[:, :J]
    y = p - 0.7 * p1 + 0.5 * f64(rs)
    return y

@@ -1,0 +1,184 @@
+from contextlib import ExitStack
+
+import concourse.mybir as mybir
+
+K, T, J, R, F, V, N = 512, 512, 256, 512, 512, 512, 256
+FLOPS = 2 * (K * R * J + F * R * J + R * N * J)
+
+F32 = mybir.dt.float32
+BF16 = mybir.dt.bfloat16
+I32 = mybir.dt.int32
+U32 = mybir.dt.uint32
+U16 = mybir.dt.uint16
+U8 = mybir.dt.uint8
+E4M3 = mybir.dt.float8_e4m3fn_x4
+E5M2 = mybir.dt.float8_e5m2_x4
+E2M1 = mybir.dt.float4_e2m1fn_x4
+ALU = mybir.AluOpType
+COPY = mybir.ActivationFunctionType.Copy
+
+P = 128
+PACK = 4
+PAD = 8
+HALF = J // 2
+
+
+def load_scales(queue, plane, scales):
+    rows = scales[0].bitcast(I32)
+    for q in range(4):
+        queue.dma_start(out=plane[32 * q : 32 * q + 4, :].bitcast(I32), in_=rows[4 * q : 4 * q + 4, :])
+
+
+def dealt(out, in_, run):
+    return (
+        out.rearrange("p (t c i) -> p c t i", t=PACK, i=run),
+        in_.rearrange("p (c i t) -> p c t i", t=PACK, i=run),
+    )
+
+
+def woven(words, planes, h):
+    cols = slice(h * HALF, (h + 1) * HALF)
+    return (
+        words[:, cols, :].rearrange("p (c i) t -> p c t i", i=4),
+        planes[:, :, cols].rearrange("p t (c i) -> p c t i", i=4),
+    )
+
+
+def quantize_half(nc, codes, scales, words, h, fmt):
+    cols = slice(h * HALF, (h + 1) * HALF)
+    nc.vector.quantize_mx(
+        out=codes[:, cols].bitcast(fmt),
+        scales=scales[:, cols],
+        in_=words[:, cols, :].rearrange("p j t -> p (j t)"),
+    )
+
+
+def tile_list_sum_steps_own_overtable_lagged_kernel(
+    tc, xf, fk, w_words, w_scales, sx_words, sx_scales, w2_words, w2_scales, tb, wb_words, wb_scales, rs, offs, offs2, out
+):
+    nc = tc.nc
+    with ExitStack() as ctx:
+        sb = ctx.enter_context(tc.tile_pool(name="sb", bufs=1))
+        ps = ctx.enter_context(tc.psum_pool(name="ps", bufs=1))
+
+        offs_sb = sb.tile([P, J // 16], U16)
+        offs2_sb = sb.tile([P, J // 16], U16)
+        fk_sb = sb.tile([P, PACK], F32)
+        xf_sb = [sb.tile([P, T], F32, name="xf%d" % t) for t in range(PACK)]
+        tb_sb = [sb.tile([P, V], F32, name="tb%d" % t) for t in range(PACK)]
+        w_raw = sb.tile([P, 2 * R], U8, align_bytes=64)
+        w2_raw = sb.tile([P, R], U32, align_bytes=64)
+        ws_raw = sb.tile([P, R], U8, align_bytes=64)
+        w2s_raw = sb.tile([P, R], U8, align_bytes=64)
+        sx_sb = sb.tile([P, J], U32, align_bytes=64)
+        sxs_sb = sb.tile([P, J], U8, align_bytes=64)
+        wb_sb = sb.tile([P, N], U32, align_bytes=64)
+        wbs_sb = sb.tile([P, N], U8, align_bytes=64)
+        rs_sb = sb.tile([P, N // P, J], F32)
+
+        xf_planes = xf.rearrange("(p t) c -> p t c", t=PACK)
+        tb_planes = tb.rearrange("(p t) c -> p t c", t=PACK)
+
+        def words_of(dram):
+            return dram[0].rearrange("p c t -> p (c t)").bitcast(I32)
+
+        for plane in (ws_raw, w2s_raw):
+            nc.vector.memset(plane[:].bitcast(I32), 0)
+        for plane in (sxs_sb, wbs_sb):
+            nc.gpsimd.memset(plane[:].bitcast(I32), 0)
+        nc.sync.dma_start(out=xf_sb[0][:], in_=xf_planes[:, 0, :])
+        nc.sync.dma_start(offs_sb[:], offs)
+        nc.scalar.dma_start(out=fk_sb[:], in_=fk.rearrange("(p t) o -> p (t o)", t=PACK))
+        for t in range(1, PACK):
+            nc.sync.dma_start(out=xf_sb[t][:], in_=xf_planes[:, t, :])
+        load_scales(nc.scalar, ws_raw, w_scales)
+        load_scales(nc.scalar, w2s_raw, w2_scales)
+        load_scales(nc.gpsimd, sxs_sb, sx_scales)
+        nc.sync.dma_start(out=w_raw[:].bitcast(I32), in_=w_words[0].bitcast(I32))
+        nc.sync.dma_start(out=w2_raw[:].bitcast(I32), in_=words_of(w2_words))
+        nc.sync.dma_start(offs2_sb[:], offs2)
+        nc.sync.dma_start(out=sx_sb[:].bitcast(I32), in_=words_of(sx_words))
+        for t in range(PACK):
+            nc.sync.dma_start(out=tb_sb[t][:], in_=tb_planes[:, t, :])
+        nc.sync.dma_start(out=wb_sb[:].bitcast(I32), in_=words_of(wb_words))
+        load_scales(nc.sync, wbs_sb, wb_scales)
+        nc.sync.dma_start(out=rs_sb[:], in_=rs.rearrange("(h p) j -> p h j", p=P))
+
+        xs = sb.tile([P, PACK, PAD + J], F32)
+        nc.vector.memset(xs[:, :, PAD - 1 : PAD], 0.0)
+        fk_wide = sb.tile([P, 2, J], F32)
+        for i in range(2):
+            t = 2 * i + 1
+            nc.vector.tensor_copy(out=fk_wide[:, i, :], in_=fk_sb[:, t : t + 1].to_broadcast([P, J]))
+        ws_sb = sb.tile([P, R], U8, align_bytes=64)
+        w2s_sb = sb.tile([P, R], U8, align_bytes=64)
+        nc.vector.tensor_copy(*dealt(ws_sb[:], ws_raw[:], 16))
+        nc.vector.tensor_copy(*dealt(w2s_sb[:], w2s_raw[:], 16))
+
+        xg = sb.tile([P, 2, J], F32)
+        u32 = sb.tile([P, PACK, J], F32)
+        for t in range(PACK):
+            picked = xf_sb[t][:].indirect(offs_sb[:])
+            if t % 2 == 0:
+                nc.scalar.activation(xg[:, t // 2, :], picked, COPY)
+                nc.scalar.activation(xs[:, t, PAD:], xg[:, t // 2, :], COPY, scale=fk_sb[:, t : t + 1])
+            else:
+                nc.vector.tensor_tensor(xs[:, t, PAD:], picked, fk_wide[:, t // 2, :], ALU.mult)
+        for t in range(PACK):
+            nc.vector.scalar_tensor_tensor(
+                u32[:, t, :], xs[:, t, PAD - 1 : PAD - 1 + J], -0.6, xs[:, t, PAD:], ALU.mult, ALU.add
+            )
+        u16 = sb.tile([P, J, PACK], BF16, align_bytes=64)
+        uq = sb.tile([P, J], U32, align_bytes=64)
+        uqs = sb.tile([P, J], U8, align_bytes=64)
+        for h in range(2):
+            nc.vector.tensor_copy(*woven(u16, u32, h))
+        for h in range(2):
+            quantize_half(nc, uq, uqs, u16, h, E4M3)
+
+        w_sb = sb.tile([P, 2 * R], U8, align_bytes=64)
+        w2_sb = sb.tile([P, R], U32, align_bytes=64)
+        nc.scalar.copy(*dealt(w_sb[:].bitcast(U16), w_raw[:].bitcast(U16), 8))
+        nc.scalar.copy(*dealt(w2_sb[:], w2_raw[:], 4))
+
+        acc = [ps.tile([P, J], F32, name="acc%d" % t) for t in range(PACK)]
+        for t in range(PACK):
+            cols = slice(t * P, (t + 1) * P)
+            nc.tensor.matmul_mx(
+                out=acc[t][:], lhsT=w2_sb[:, cols].bitcast(E5M2), lhsT_scale=w2s_sb[:, cols],
+                rhs=sx_sb[:].bitcast(E4M3), rhs_scale=sxs_sb[:], start=True, stop=False,
+            )
+        for t in range(PACK):
+            cols = slice(t * P, (t + 1) * P)
+            nc.tensor.matmul_mx(
+                out=acc[t][:], lhsT=w_sb[:, 2 * t * P : 2 * (t + 1) * P].bitcast(E2M1), lhsT_scale=ws_sb[:, cols],
+                rhs=uq[:].bitcast(E4M3), rhs_scale=uqs[:], start=False, stop=True,
+            )
+
+        tg = sb.tile([P, PACK, J], F32)
+        pre = sb.tile([P, PACK, J], F32)
+        for t in range(PACK):
+            nc.scalar.activation(tg[:, t, :], tb_sb[t][:].indirect(offs2_sb[:]), COPY)
+            nc.vector.tensor_tensor(pre[:, t, :], acc[t][:], tg[:, t, :], ALU.subtract)
+        h16 = sb.tile([P, J, PACK], BF16, align_bytes=64)
+        hq = sb.tile([P, J], U32, align_bytes=64)
+        hqs = sb.tile([P, J], U8, align_bytes=64)
+        for h in range(2):
+            dst, src = woven(h16, pre, h)
+            nc.vector.tensor_scalar(dst, src, 0.0, None, ALU.max)
+        for h in range(2):
+            quantize_half(nc, hq, hqs, h16, h, E5M2)
+
+        prod = [ps.tile([P, J], F32, name="prod%d" % g) for g in range(N // P)]
+        y = [sb.tile([P, J], F32, name="y%d" % g) for g in range(N // P)]
+        for g in range(N // P):
+            cols = slice(g * P, (g + 1) * P)
+            nc.tensor.matmul_mx(
+                out=prod[g][:], lhsT=wb_sb[:, cols].bitcast(E5M2), lhsT_scale=wbs_sb[:, cols],
+                rhs=hq[:].bitcast(E5M2), rhs_scale=hqs[:], start=True, stop=True,
+            )
+        for g in range(N // P):
+            nc.vector.scalar_tensor_tensor(y[g][:], rs_sb[:, g, :], 0.5, prod[g][:], ALU.mult, ALU.add)
+        for g in range(N // P):
+            nc.vector.scalar_tensor_tensor(y[g][:, 1:], prod[g][:, : J - 1], -0.7, y[g][:, 1:], ALU.mult, ALU.add)
+            nc.sync.dma_start(out=out[g * P : (g + 1) * P, :], in_=y[g][:])

@@ -16,16 +16,18 @@ E5M2 = mybir.dt.float8_e5m2_x4
 E2M1 = mybir.dt.float4_e2m1fn_x4
 ALU = mybir.AluOpType
 COPY = mybir.ActivationFunctionType.Copy
+RELU = mybir.ActivationFunctionType.Relu
 
 P = 128
 PACK = 4
 PAD = 8
 HALF = J // 2
+SPLIT = 160
 
 
-def load_scales(queue, plane, scales):
+def load_scales(queue, plane, scales, quarters):
     rows = scales[0].bitcast(I32)
-    for q in range(4):
+    for q in quarters:
         queue.dma_start(out=plane[32 * q : 32 * q + 4, :].bitcast(I32), in_=rows[4 * q : 4 * q + 4, :])
 
 
@@ -36,8 +38,7 @@ def dealt(out, in_, run):
     )
 
 
-def woven(words, planes, h):
-    cols = slice(h * HALF, (h + 1) * HALF)
+def woven(words, planes, cols):
     return (
         words[:, cols, :].rearrange("p (c i) t -> p c t i", i=4),
         planes[:, :, cols].rearrange("p t (c i) -> p c t i", i=4),
@@ -68,10 +69,10 @@ def tile_list_sum_steps_own_overtable_lagged_kernel(
         tb_sb = [sb.tile([P, V], F32, name="tb%d" % t) for t in range(PACK)]
         w_raw = sb.tile([P, 2 * R], U8, align_bytes=64)
         w2_raw = sb.tile([P, R], U32, align_bytes=64)
-        ws_raw = sb.tile([P, R], U8, align_bytes=64)
-        w2s_raw = sb.tile([P, R], U8, align_bytes=64)
+        raw = sb.tile([P, 2, R], U8, align_bytes=64)
+        planes = sb.tile([P, 2 * R + J], U8, align_bytes=64)
+        w2s_sb, ws_sb, sxs_sb = planes[:, 0:R], planes[:, R : 2 * R], planes[:, 2 * R :]
         sx_sb = sb.tile([P, J], U32, align_bytes=64)
-        sxs_sb = sb.tile([P, J], U8, align_bytes=64)
         wb_sb = sb.tile([P, N], U32, align_bytes=64)
         wbs_sb = sb.tile([P, N], U8, align_bytes=64)
         rs_sb = sb.tile([P, N // P, J], F32)
@@ -82,38 +83,34 @@ def tile_list_sum_steps_own_overtable_lagged_kernel(
         def words_of(dram):
             return dram[0].rearrange("p c t -> p (c t)").bitcast(I32)
 
-        for plane in (ws_raw, w2s_raw):
-            nc.vector.memset(plane[:].bitcast(I32), 0)
-        for plane in (sxs_sb, wbs_sb):
-            nc.gpsimd.memset(plane[:].bitcast(I32), 0)
-        nc.sync.dma_start(out=xf_sb[0][:], in_=xf_planes[:, 0, :])
+        nc.scalar.dma_start(out=raw[112:128, 0, :].bitcast(I32), in_=w2_scales[0].bitcast(I32))
+        nc.scalar.dma_start(out=raw[112:128, 1, :].bitcast(I32), in_=w_scales[0].bitcast(I32))
+        nc.scalar.dma_start(out=sxs_sb[112:128, :].bitcast(I32), in_=sx_scales[0].bitcast(I32))
+        nc.vector.memset(raw[0:112].rearrange("p s c -> p (s c)").bitcast(I32), 0)
         nc.sync.dma_start(offs_sb[:], offs)
-        nc.scalar.dma_start(out=fk_sb[:], in_=fk.rearrange("(p t) o -> p (t o)", t=PACK))
-        for t in range(1, PACK):
-            nc.sync.dma_start(out=xf_sb[t][:], in_=xf_planes[:, t, :])
-        load_scales(nc.scalar, ws_raw, w_scales)
-        load_scales(nc.scalar, w2s_raw, w2_scales)
-        load_scales(nc.gpsimd, sxs_sb, sx_scales)
-        nc.sync.dma_start(out=w_raw[:].bitcast(I32), in_=w_words[0].bitcast(I32))
-        nc.sync.dma_start(out=w2_raw[:].bitcast(I32), in_=words_of(w2_words))
-        nc.sync.dma_start(offs2_sb[:], offs2)
-        nc.sync.dma_start(out=sx_sb[:].bitcast(I32), in_=words_of(sx_words))
+        nc.sync.dma_start(out=fk_sb[:], in_=fk.rearrange("(p t) o -> p (t o)", t=PACK))
         for t in range(PACK):
+            nc.sync.dma_start(out=xf_sb[t][:], in_=xf_planes[:, t, :])
+        nc.vector.tensor_copy(*dealt(w2s_sb, raw[:, 0, :], 16))
+        nc.vector.tensor_copy(*dealt(ws_sb, raw[:, 1, :], 16))
+        for q in range(4):
+            nc.sync.dma_start(out=planes[32 * q : 32 * q + 4, :].bitcast(I32), in_=planes[112 + 4 * q : 116 + 4 * q, :].bitcast(I32))
+        nc.sync.dma_start(out=w2_raw[:].bitcast(I32), in_=words_of(w2_words))
+        nc.sync.dma_start(out=w_raw[:].bitcast(I32), in_=w_words[0].bitcast(I32))
+        nc.sync.dma_start(out=sx_sb[:].bitcast(I32), in_=words_of(sx_words))
+        nc.sync.dma_start(out=tb_sb[0][:], in_=tb_planes[:, 0, :])
+        nc.sync.dma_start(offs2_sb[:], offs2)
+        for t in range(1, PACK):
             nc.sync.dma_start(out=tb_sb[t][:], in_=tb_planes[:, t, :])
         nc.sync.dma_start(out=wb_sb[:].bitcast(I32), in_=words_of(wb_words))
-        load_scales(nc.sync, wbs_sb, wb_scales)
+        load_scales(nc.sync, wbs_sb, wb_scales, (0, 1, 2, 3))
         nc.sync.dma_start(out=rs_sb[:], in_=rs.rearrange("(h p) j -> p h j", p=P))
 
         xs = sb.tile([P, PACK, PAD + J], F32)
         nc.vector.memset(xs[:, :, PAD - 1 : PAD], 0.0)
         fk_wide = sb.tile([P, 2, J], F32)
-        for i in range(2):
-            t = 2 * i + 1
-            nc.vector.tensor_copy(out=fk_wide[:, i, :], in_=fk_sb[:, t : t + 1].to_broadcast([P, J]))
-        ws_sb = sb.tile([P, R], U8, align_bytes=64)
-        w2s_sb = sb.tile([P, R], U8, align_bytes=64)
-        nc.vector.tensor_copy(*dealt(ws_sb[:], ws_raw[:], 16))
-        nc.vector.tensor_copy(*dealt(w2s_sb[:], w2s_raw[:], 16))
+        nc.scalar.activation(fk_wide[:, 0, :], fk_sb[:, 1:2].to_broadcast([P, J]), COPY)
+        nc.vector.tensor_copy(out=fk_wide[:, 1, :], in_=fk_sb[:, 3:4].to_broadcast([P, J]))
 
         xg = sb.tile([P, 2, J], F32)
         u32 = sb.tile([P, PACK, J], F32)
@@ -132,21 +129,21 @@ def tile_list_sum_steps_own_overtable_lagged_kernel(
         uq = sb.tile([P, J], U32, align_bytes=64)
         uqs = sb.tile([P, J], U8, align_bytes=64)
         for h in range(2):
-            nc.vector.tensor_copy(*woven(u16, u32, h))
+            nc.vector.tensor_copy(*woven(u16, u32, slice(h * HALF, (h + 1) * HALF)))
         for h in range(2):
             quantize_half(nc, uq, uqs, u16, h, E4M3)
 
         w_sb = sb.tile([P, 2 * R], U8, align_bytes=64)
         w2_sb = sb.tile([P, R], U32, align_bytes=64)
-        nc.scalar.copy(*dealt(w_sb[:].bitcast(U16), w_raw[:].bitcast(U16), 8))
         nc.scalar.copy(*dealt(w2_sb[:], w2_raw[:], 4))
+        nc.scalar.copy(*dealt(w_sb[:].bitcast(U16), w_raw[:].bitcast(U16), 8))
 
         acc = [ps.tile([P, J], F32, name="acc%d" % t) for t in range(PACK)]
         for t in range(PACK):
             cols = slice(t * P, (t + 1) * P)
             nc.tensor.matmul_mx(
                 out=acc[t][:], lhsT=w2_sb[:, cols].bitcast(E5M2), lhsT_scale=w2s_sb[:, cols],
-                rhs=sx_sb[:].bitcast(E4M3), rhs_scale=sxs_sb[:], start=True, stop=False,
+                rhs=sx_sb[:].bitcast(E4M3), rhs_scale=sxs_sb, start=True, stop=False,
             )
         for t in range(PACK):
             cols = slice(t * P, (t + 1) * P)
@@ -163,20 +160,23 @@ def tile_list_sum_steps_own_overtable_lagged_kernel(
         h16 = sb.tile([P, J, PACK], BF16, align_bytes=64)
         hq = sb.tile([P, J], U32, align_bytes=64)
         hqs = sb.tile([P, J], U8, align_bytes=64)
-        for h in range(2):
-            dst, src = woven(h16, pre, h)
-            nc.vector.tensor_scalar(dst, src, 0.0, None, ALU.max)
+        dst, src = woven(h16, pre, slice(0, SPLIT))
+        nc.vector.tensor_scalar(dst, src, 0.0, None, ALU.max)
+        dst, src = woven(h16, pre, slice(SPLIT, J))
+        nc.scalar.activation(dst, src, RELU)
         for h in range(2):
             quantize_half(nc, hq, hqs, h16, h, E5M2)
 
         prod = [ps.tile([P, J], F32, name="prod%d" % g) for g in range(N // P)]
         y = [sb.tile([P, J], F32, name="y%d" % g) for g in range(N // P)]
-        for g in range(N // P):
-            cols = slice(g * P, (g + 1) * P)
-            nc.tensor.matmul_mx(
-                out=prod[g][:], lhsT=wb_sb[:, cols].bitcast(E5M2), lhsT_scale=wbs_sb[:, cols],
-                rhs=hq[:].bitcast(E5M2), rhs_scale=hqs[:], start=True, stop=True,
-            )
+        for h in range(2):
+            half = slice(h * HALF, (h + 1) * HALF)
+            for g in range(N // P):
+                cols = slice(g * P, (g + 1) * P)
+                nc.tensor.matmul_mx(
+                    out=prod[g][:, half], lhsT=wb_sb[:, cols].bitcast(E5M2), lhsT_scale=wbs_sb[:, cols],
+                    rhs=hq[:, half].bitcast(E5M2), rhs_scale=hqs[:, half], start=True, stop=True,
+                )
         for g in range(N // P):
             nc.vector.scalar_tensor_tensor(y[g][:], rs_sb[:, g, :], 0.5, prod[g][:], ALU.mult, ALU.add)
         for g in range(N // P):

@@ -22,7 +22,8 @@ P = 128
 PACK = 4
 PAD = 8
 HALF = J // 2
-SPLIT = 160
+HALVES = (slice(0, HALF), slice(HALF, J))
+SPLIT = 192
 
 
 def load_scales(queue, plane, scales, quarters):
@@ -66,10 +67,13 @@ def tile_list_sum_steps_own_overtable_lagged_kernel(
         offs2_sb = sb.tile([P, J // 16], U16)
         fk_sb = sb.tile([P, PACK], F32)
         xf_sb = [sb.tile([P, T], F32, name="xf%d" % t) for t in range(PACK)]
-        tb_sb = [sb.tile([P, V], F32, name="tb%d" % t) for t in range(PACK)]
+        tb_first = sb.tile([P, 2, V], F32)
+        tb_rest = [sb.tile([P, V], F32, name="tb%d" % t) for t in range(2, PACK)]
+        tb_sb = [tb_first[:, 0, :], tb_first[:, 1, :], tb_rest[0][:], tb_rest[1][:]]
         w_raw = sb.tile([P, 2 * R], U8, align_bytes=64)
         w2_raw = sb.tile([P, R], U32, align_bytes=64)
-        raw = sb.tile([P, 2, R], U8, align_bytes=64)
+        ws_raw = sb.tile([P, R], U8, align_bytes=64)
+        w2s_raw = sb.tile([P, R], U8, align_bytes=64)
         planes = sb.tile([P, 2 * R + J], U8, align_bytes=64)
         w2s_sb, ws_sb, sxs_sb = planes[:, 0:R], planes[:, R : 2 * R], planes[:, 2 * R :]
         sx_sb = sb.tile([P, J], U32, align_bytes=64)
@@ -83,25 +87,25 @@ def tile_list_sum_steps_own_overtable_lagged_kernel(
         def words_of(dram):
             return dram[0].rearrange("p c t -> p (c t)").bitcast(I32)
 
-        nc.scalar.dma_start(out=raw[112:128, 0, :].bitcast(I32), in_=w2_scales[0].bitcast(I32))
-        nc.scalar.dma_start(out=raw[112:128, 1, :].bitcast(I32), in_=w_scales[0].bitcast(I32))
-        nc.scalar.dma_start(out=sxs_sb[112:128, :].bitcast(I32), in_=sx_scales[0].bitcast(I32))
-        nc.vector.memset(raw[0:112].rearrange("p s c -> p (s c)").bitcast(I32), 0)
+        for raw, scales in ((w2s_raw, w2_scales), (ws_raw, w_scales)):
+            rows = scales[0].bitcast(I32).unsqueeze(1).broadcast_to([16, 8, R // 4])
+            nc.scalar.dma_start(out=raw[:].bitcast(I32), in_=rows)
+        nc.scalar.dma_start(out=sxs_sb[0:P:8, :].bitcast(I32), in_=sx_scales[0].bitcast(I32))
         nc.sync.dma_start(offs_sb[:], offs)
         nc.sync.dma_start(out=fk_sb[:], in_=fk.rearrange("(p t) o -> p (t o)", t=PACK))
         for t in range(PACK):
             nc.sync.dma_start(out=xf_sb[t][:], in_=xf_planes[:, t, :])
-        nc.vector.tensor_copy(*dealt(w2s_sb, raw[:, 0, :], 16))
-        nc.vector.tensor_copy(*dealt(ws_sb, raw[:, 1, :], 16))
-        for q in range(4):
-            nc.sync.dma_start(out=planes[32 * q : 32 * q + 4, :].bitcast(I32), in_=planes[112 + 4 * q : 116 + 4 * q, :].bitcast(I32))
+        nc.vector.tensor_copy(*dealt(w2s_sb, w2s_raw[:], 16))
+        nc.vector.tensor_copy(*dealt(ws_sb, ws_raw[:], 16))
         nc.sync.dma_start(out=w2_raw[:].bitcast(I32), in_=words_of(w2_words))
         nc.sync.dma_start(out=w_raw[:].bitcast(I32), in_=w_words[0].bitcast(I32))
         nc.sync.dma_start(out=sx_sb[:].bitcast(I32), in_=words_of(sx_words))
-        nc.sync.dma_start(out=tb_sb[0][:], in_=tb_planes[:, 0, :])
+        for r in range(1, 4):
+            nc.sync.dma_start(out=planes[r:P:32, :].bitcast(I32), in_=planes[8 * r : P : 32, :].bitcast(I32))
+        nc.sync.dma_start(out=tb_first[:], in_=tb_planes[:, 0:2, :])
         nc.sync.dma_start(offs2_sb[:], offs2)
-        for t in range(1, PACK):
-            nc.sync.dma_start(out=tb_sb[t][:], in_=tb_planes[:, t, :])
+        for t in range(2, PACK):
+            nc.sync.dma_start(out=tb_sb[t], in_=tb_planes[:, t, :])
         nc.sync.dma_start(out=wb_sb[:].bitcast(I32), in_=words_of(wb_words))
         load_scales(nc.sync, wbs_sb, wb_scales, (0, 1, 2, 3))
         nc.sync.dma_start(out=rs_sb[:], in_=rs.rearrange("(h p) j -> p h j", p=P))
@@ -121,9 +125,9 @@ def tile_list_sum_steps_own_overtable_lagged_kernel(
                 nc.scalar.activation(xs[:, t, PAD:], xg[:, t // 2, :], COPY, scale=fk_sb[:, t : t + 1])
             else:
                 nc.vector.tensor_tensor(xs[:, t, PAD:], picked, fk_wide[:, t // 2, :], ALU.mult)
-        for t in range(PACK):
+        for ts in (slice(0, 1), slice(1, 2), slice(2, 4)):
             nc.vector.scalar_tensor_tensor(
-                u32[:, t, :], xs[:, t, PAD - 1 : PAD - 1 + J], -0.6, xs[:, t, PAD:], ALU.mult, ALU.add
+                u32[:, ts, :], xs[:, ts, PAD - 1 : PAD - 1 + J], -0.6, xs[:, ts, PAD:], ALU.mult, ALU.add
             )
         u16 = sb.tile([P, J, PACK], BF16, align_bytes=64)
         uq = sb.tile([P, J], U32, align_bytes=64)
@@ -154,31 +158,45 @@ def tile_list_sum_steps_own_overtable_lagged_kernel(
 
         tg = sb.tile([P, PACK, J], F32)
         pre = sb.tile([P, PACK, J], F32)
-        for t in range(PACK):
-            nc.scalar.activation(tg[:, t, :], tb_sb[t][:].indirect(offs2_sb[:]), COPY)
+        last = PACK - 1
+        for t in range(last):
+            picked = tb_sb[t].indirect(offs2_sb[:])
+            if t == 0:
+                nc.vector.tensor_copy(tg[:, t, :], picked)
+            else:
+                nc.scalar.activation(tg[:, t, :], picked, COPY)
             nc.vector.tensor_tensor(pre[:, t, :], acc[t][:], tg[:, t, :], ALU.subtract)
         h16 = sb.tile([P, J, PACK], BF16, align_bytes=64)
+        for h, half in enumerate(HALVES):
+            nc.scalar.activation(tg[:, last, half], tb_sb[last].indirect(offs2_sb[:, 8 * h : 8 * h + 8]), COPY)
+            nc.vector.tensor_tensor(pre[:, last, half], acc[last][:, half], tg[:, last, half], ALU.subtract)
+            if h == 0:
+                dst, src = woven(h16, pre, half)
+                nc.vector.tensor_scalar(dst, src, 0.0, None, ALU.max)
         hq = sb.tile([P, J], U32, align_bytes=64)
         hqs = sb.tile([P, J], U8, align_bytes=64)
-        dst, src = woven(h16, pre, slice(0, SPLIT))
+        quantize_half(nc, hq, hqs, h16, 0, E5M2)
+        dst, src = woven(h16, pre, slice(HALF, SPLIT))
         nc.vector.tensor_scalar(dst, src, 0.0, None, ALU.max)
         dst, src = woven(h16, pre, slice(SPLIT, J))
         nc.scalar.activation(dst, src, RELU)
-        for h in range(2):
-            quantize_half(nc, hq, hqs, h16, h, E5M2)
+        quantize_half(nc, hq, hqs, h16, 1, E5M2)
 
-        prod = [ps.tile([P, J], F32, name="prod%d" % g) for g in range(N // P)]
-        y = [sb.tile([P, J], F32, name="y%d" % g) for g in range(N // P)]
-        for h in range(2):
-            half = slice(h * HALF, (h + 1) * HALF)
+        out_rows = out.rearrange("(g p) j -> p g j", p=P)
+        prod = [ps.tile([P, N // P, HALF], F32, name="prod%d" % h) for h in range(2)]
+        y = [sb.tile([P, N // P, HALF], F32, name="y%d" % h) for h in range(2)]
+        for h, half in enumerate(HALVES):
             for g in range(N // P):
                 cols = slice(g * P, (g + 1) * P)
                 nc.tensor.matmul_mx(
-                    out=prod[g][:, half], lhsT=wb_sb[:, cols].bitcast(E5M2), lhsT_scale=wbs_sb[:, cols],
+                    out=prod[h][:, g, :], lhsT=wb_sb[:, cols].bitcast(E5M2), lhsT_scale=wbs_sb[:, cols],
                     rhs=hq[:, half].bitcast(E5M2), rhs_scale=hqs[:, half], start=True, stop=True,
                 )
-        for g in range(N // P):
-            nc.vector.scalar_tensor_tensor(y[g][:], rs_sb[:, g, :], 0.5, prod[g][:], ALU.mult, ALU.add)
-        for g in range(N // P):
-            nc.vector.scalar_tensor_tensor(y[g][:, 1:], prod[g][:, : J - 1], -0.7, y[g][:, 1:], ALU.mult, ALU.add)
-            nc.sync.dma_start(out=out[g * P : (g + 1) * P, :], in_=y[g][:])
+        for h, half in enumerate(HALVES):
+            nxt = slice(half.start + 1, min(half.stop + 1, J))
+            nc.vector.scalar_tensor_tensor(
+                rs_sb[:, :, nxt], prod[h][:, :, : nxt.stop - nxt.start], -1.4, rs_sb[:, :, nxt], ALU.mult, ALU.add
+            )
+        for h, half in enumerate(HALVES):
+            nc.vector.scalar_tensor_tensor(y[h][:], rs_sb[:, :, half], 0.5, prod[h][:], ALU.mult, ALU.add)
+            nc.sync.dma_start(out=out_rows[:, :, half], in_=y[h][:])

@@ -23,7 +23,7 @@ PACK = 4
 PAD = 8
 HALF = J // 2
 HALVES = (slice(0, HALF), slice(HALF, J))
-SPLIT = 192
+SPLIT = 176
 
 
 def load_scales(queue, plane, scales, quarters):
@@ -72,8 +72,7 @@ def tile_list_sum_steps_own_overtable_lagged_kernel(
         tb_sb = [tb_first[:, 0, :], tb_first[:, 1, :], tb_rest[0][:], tb_rest[1][:]]
         w_raw = sb.tile([P, 2 * R], U8, align_bytes=64)
         w2_raw = sb.tile([P, R], U32, align_bytes=64)
-        ws_raw = sb.tile([P, R], U8, align_bytes=64)
-        w2s_raw = sb.tile([P, R], U8, align_bytes=64)
+        raw = sb.tile([P, 2, R], U8, align_bytes=64)
         planes = sb.tile([P, 2 * R + J], U8, align_bytes=64)
         w2s_sb, ws_sb, sxs_sb = planes[:, 0:R], planes[:, R : 2 * R], planes[:, 2 * R :]
         sx_sb = sb.tile([P, J], U32, align_bytes=64)
@@ -87,21 +86,21 @@ def tile_list_sum_steps_own_overtable_lagged_kernel(
         def words_of(dram):
             return dram[0].rearrange("p c t -> p (c t)").bitcast(I32)
 
-        for raw, scales in ((w2s_raw, w2_scales), (ws_raw, w_scales)):
-            rows = scales[0].bitcast(I32).unsqueeze(1).broadcast_to([16, 8, R // 4])
-            nc.scalar.dma_start(out=raw[:].bitcast(I32), in_=rows)
-        nc.scalar.dma_start(out=sxs_sb[0:P:8, :].bitcast(I32), in_=sx_scales[0].bitcast(I32))
+        nc.scalar.dma_start(out=raw[112:128, 0, :].bitcast(I32), in_=w2_scales[0].bitcast(I32))
+        nc.scalar.dma_start(out=raw[112:128, 1, :].bitcast(I32), in_=w_scales[0].bitcast(I32))
+        nc.scalar.dma_start(out=sxs_sb[112:128, :].bitcast(I32), in_=sx_scales[0].bitcast(I32))
+        nc.vector.memset(raw[0:112].rearrange("p s c -> p (s c)").bitcast(I32), 0)
         nc.sync.dma_start(offs_sb[:], offs)
         nc.sync.dma_start(out=fk_sb[:], in_=fk.rearrange("(p t) o -> p (t o)", t=PACK))
         for t in range(PACK):
             nc.sync.dma_start(out=xf_sb[t][:], in_=xf_planes[:, t, :])
-        nc.vector.tensor_copy(*dealt(w2s_sb, w2s_raw[:], 16))
-        nc.vector.tensor_copy(*dealt(ws_sb, ws_raw[:], 16))
+        nc.vector.tensor_copy(*dealt(w2s_sb, raw[:, 0, :], 16))
+        nc.vector.tensor_copy(*dealt(ws_sb, raw[:, 1, :], 16))
         nc.sync.dma_start(out=w2_raw[:].bitcast(I32), in_=words_of(w2_words))
-        nc.sync.dma_start(out=w_raw[:].bitcast(I32), in_=w_words[0].bitcast(I32))
         nc.sync.dma_start(out=sx_sb[:].bitcast(I32), in_=words_of(sx_words))
-        for r in range(1, 4):
-            nc.sync.dma_start(out=planes[r:P:32, :].bitcast(I32), in_=planes[8 * r : P : 32, :].bitcast(I32))
+        for q in range(4):
+            nc.sync.dma_start(out=planes[32 * q : 32 * q + 4, :].bitcast(I32), in_=planes[112 + 4 * q : 116 + 4 * q, :].bitcast(I32))
+        nc.sync.dma_start(out=w_raw[:].bitcast(I32), in_=w_words[0].bitcast(I32))
         nc.sync.dma_start(out=tb_first[:], in_=tb_planes[:, 0:2, :])
         nc.sync.dma_start(offs2_sb[:], offs2)
         for t in range(2, PACK):
@@ -132,14 +131,14 @@ def tile_list_sum_steps_own_overtable_lagged_kernel(
         u16 = sb.tile([P, J, PACK], BF16, align_bytes=64)
         uq = sb.tile([P, J], U32, align_bytes=64)
         uqs = sb.tile([P, J], U8, align_bytes=64)
-        for h in range(2):
-            nc.vector.tensor_copy(*woven(u16, u32, slice(h * HALF, (h + 1) * HALF)))
-        for h in range(2):
-            quantize_half(nc, uq, uqs, u16, h, E4M3)
-
         w_sb = sb.tile([P, 2 * R], U8, align_bytes=64)
         w2_sb = sb.tile([P, R], U32, align_bytes=64)
         nc.scalar.copy(*dealt(w2_sb[:], w2_raw[:], 4))
+        nc.vector.tensor_copy(*woven(u16, u32, HALVES[0]))
+        nc.vector.tensor_copy(*woven(u16, u32, slice(HALF, SPLIT)))
+        nc.scalar.copy(*woven(u16, u32, slice(SPLIT, J)))
+        for h in range(2):
+            quantize_half(nc, uq, uqs, u16, h, E4M3)
         nc.scalar.copy(*dealt(w_sb[:].bitcast(U16), w_raw[:].bitcast(U16), 8))
 
         acc = [ps.tile([P, J], F32, name="acc%d" % t) for t in range(PACK)]
@@ -170,17 +169,15 @@ def tile_list_sum_steps_own_overtable_lagged_kernel(
         for h, half in enumerate(HALVES):
             nc.scalar.activation(tg[:, last, half], tb_sb[last].indirect(offs2_sb[:, 8 * h : 8 * h + 8]), COPY)
             nc.vector.tensor_tensor(pre[:, last, half], acc[last][:, half], tg[:, last, half], ALU.subtract)
-            if h == 0:
-                dst, src = woven(h16, pre, half)
-                nc.vector.tensor_scalar(dst, src, 0.0, None, ALU.max)
         hq = sb.tile([P, J], U32, align_bytes=64)
         hqs = sb.tile([P, J], U8, align_bytes=64)
-        quantize_half(nc, hq, hqs, h16, 0, E5M2)
-        dst, src = woven(h16, pre, slice(HALF, SPLIT))
-        nc.vector.tensor_scalar(dst, src, 0.0, None, ALU.max)
+        for cols in (HALVES[0], slice(HALF, SPLIT)):
+            dst, src = woven(h16, pre, cols)
+            nc.vector.tensor_scalar(dst, src, 0.0, None, ALU.max)
         dst, src = woven(h16, pre, slice(SPLIT, J))
         nc.scalar.activation(dst, src, RELU)
-        quantize_half(nc, hq, hqs, h16, 1, E5M2)
+        for h in range(2):
+            quantize_half(nc, hq, hqs, h16, h, E5M2)
 
         out_rows = out.rearrange("(g p) j -> p g j", p=P)
         prod = [ps.tile([P, N // P, HALF], F32, name="prod%d" % h) for h in range(2)]

from contextlib import ExitStack

import concourse.mybir as mybir

K, T, J, R, F, V, N = 512, 512, 256, 512, 512, 512, 256
FLOPS = 2 * (K * R * J + F * R * J + R * N * J)

F32 = mybir.dt.float32
BF16 = mybir.dt.bfloat16
I32 = mybir.dt.int32
U32 = mybir.dt.uint32
U16 = mybir.dt.uint16
U8 = mybir.dt.uint8
E4M3 = mybir.dt.float8_e4m3fn_x4
E5M2 = mybir.dt.float8_e5m2_x4
E2M1 = mybir.dt.float4_e2m1fn_x4
ALU = mybir.AluOpType
COPY = mybir.ActivationFunctionType.Copy
RELU = mybir.ActivationFunctionType.Relu

P = 128
PACK = 4
PAD = 8
HALF = J // 2
HALVES = (slice(0, HALF), slice(HALF, J))
SPLIT = 176


def load_scales(queue, plane, scales, quarters):
    rows = scales[0].bitcast(I32)
    for q in quarters:
        queue.dma_start(out=plane[32 * q : 32 * q + 4, :].bitcast(I32), in_=rows[4 * q : 4 * q + 4, :])


def dealt(out, in_, run):
    return (
        out.rearrange("p (t c i) -> p c t i", t=PACK, i=run),
        in_.rearrange("p (c i t) -> p c t i", t=PACK, i=run),
    )


def woven(words, planes, cols):
    return (
        words[:, cols, :].rearrange("p (c i) t -> p c t i", i=4),
        planes[:, :, cols].rearrange("p t (c i) -> p c t i", i=4),
    )


def quantize_half(nc, codes, scales, words, h, fmt):
    cols = slice(h * HALF, (h + 1) * HALF)
    nc.vector.quantize_mx(
        out=codes[:, cols].bitcast(fmt),
        scales=scales[:, cols],
        in_=words[:, cols, :].rearrange("p j t -> p (j t)"),
    )


def tile_list_sum_steps_own_overtable_lagged_kernel(
    tc, xf, fk, w_words, w_scales, sx_words, sx_scales, w2_words, w2_scales, tb, wb_words, wb_scales, rs, offs, offs2, out
):
    nc = tc.nc
    with ExitStack() as ctx:
        sb = ctx.enter_context(tc.tile_pool(name="sb", bufs=1))
        ps = ctx.enter_context(tc.psum_pool(name="ps", bufs=1))

        offs_sb = sb.tile([P, J // 16], U16)
        offs2_sb = sb.tile([P, J // 16], U16)
        fk_sb = sb.tile([P, PACK], F32)
        xf_sb = [sb.tile([P, T], F32, name="xf%d" % t) for t in range(PACK)]
        tb_first = sb.tile([P, 2, V], F32)
        tb_rest = [sb.tile([P, V], F32, name="tb%d" % t) for t in range(2, PACK)]
        tb_sb = [tb_first[:, 0, :], tb_first[:, 1, :], tb_rest[0][:], tb_rest[1][:]]
        w_raw = sb.tile([P, 2 * R], U8, align_bytes=64)
        w2_raw = sb.tile([P, R], U32, align_bytes=64)
        raw = sb.tile([P, 2, R], U8, align_bytes=64)
        planes = sb.tile([P, 2 * R + J], U8, align_bytes=64)
        w2s_sb, ws_sb, sxs_sb = planes[:, 0:R], planes[:, R : 2 * R], planes[:, 2 * R :]
        sx_sb = sb.tile([P, J], U32, align_bytes=64)
        wb_sb = sb.tile([P, N], U32, align_bytes=64)
        wbs_sb = sb.tile([P, N], U8, align_bytes=64)
        rs_sb = sb.tile([P, N // P, J], F32)

        xf_planes = xf.rearrange("(p t) c -> p t c", t=PACK)
        tb_planes = tb.rearrange("(p t) c -> p t c", t=PACK)

        def words_of(dram):
            return dram[0].rearrange("p c t -> p (c t)").bitcast(I32)

        nc.scalar.dma_start(out=raw[112:128, 0, :].bitcast(I32), in_=w2_scales[0].bitcast(I32))
        nc.scalar.dma_start(out=raw[112:128, 1, :].bitcast(I32), in_=w_scales[0].bitcast(I32))
        nc.scalar.dma_start(out=sxs_sb[112:128, :].bitcast(I32), in_=sx_scales[0].bitcast(I32))
        nc.vector.memset(raw[0:112].rearrange("p s c -> p (s c)").bitcast(I32), 0)
        nc.sync.dma_start(offs_sb[:], offs)
        nc.sync.dma_start(out=fk_sb[:], in_=fk.rearrange("(p t) o -> p (t o)", t=PACK))
        for t in range(PACK):
            nc.sync.dma_start(out=xf_sb[t][:], in_=xf_planes[:, t, :])
        nc.vector.tensor_copy(*dealt(w2s_sb, raw[:, 0, :], 16))
        nc.vector.tensor_copy(*dealt(ws_sb, raw[:, 1, :], 16))
        nc.sync.dma_start(out=w2_raw[:].bitcast(I32), in_=words_of(w2_words))
        nc.sync.dma_start(out=sx_sb[:].bitcast(I32), in_=words_of(sx_words))
        for q in range(4):
            nc.sync.dma_start(out=planes[32 * q : 32 * q + 4, :].bitcast(I32), in_=planes[112 + 4 * q : 116 + 4 * q, :].bitcast(I32))
        nc.sync.dma_start(out=w_raw[:].bitcast(I32), in_=w_words[0].bitcast(I32))
        nc.sync.dma_start(out=tb_first[:], in_=tb_planes[:, 0:2, :])
        nc.sync.dma_start(offs2_sb[:], offs2)
        for t in range(2, PACK):
            nc.sync.dma_start(out=tb_sb[t], in_=tb_planes[:, t, :])
        nc.sync.dma_start(out=wb_sb[:].bitcast(I32), in_=words_of(wb_words))
        load_scales(nc.sync, wbs_sb, wb_scales, (0, 1, 2, 3))
        nc.sync.dma_start(out=rs_sb[:], in_=rs.rearrange("(h p) j -> p h j", p=P))

        xs = sb.tile([P, PACK, PAD + J], F32)
        nc.vector.memset(xs[:, :, PAD - 1 : PAD], 0.0)
        fk_wide = sb.tile([P, 2, J], F32)
        nc.scalar.activation(fk_wide[:, 0, :], fk_sb[:, 1:2].to_broadcast([P, J]), COPY)
        nc.vector.tensor_copy(out=fk_wide[:, 1, :], in_=fk_sb[:, 3:4].to_broadcast([P, J]))

        xg = sb.tile([P, 2, J], F32)
        u32 = sb.tile([P, PACK, J], F32)
        for t in range(PACK):
            picked = xf_sb[t][:].indirect(offs_sb[:])
            if t % 2 == 0:
                nc.scalar.activation(xg[:, t // 2, :], picked, COPY)
                nc.scalar.activation(xs[:, t, PAD:], xg[:, t // 2, :], COPY, scale=fk_sb[:, t : t + 1])
            else:
                nc.vector.tensor_tensor(xs[:, t, PAD:], picked, fk_wide[:, t // 2, :], ALU.mult)
        for ts in (slice(0, 1), slice(1, 2), slice(2, 4)):
            nc.vector.scalar_tensor_tensor(
                u32[:, ts, :], xs[:, ts, PAD - 1 : PAD - 1 + J], -0.6, xs[:, ts, PAD:], ALU.mult, ALU.add
            )
        u16 = sb.tile([P, J, PACK], BF16, align_bytes=64)
        uq = sb.tile([P, J], U32, align_bytes=64)
        uqs = sb.tile([P, J], U8, align_bytes=64)
        w_sb = sb.tile([P, 2 * R], U8, align_bytes=64)
        w2_sb = sb.tile([P, R], U32, align_bytes=64)
        nc.scalar.copy(*dealt(w2_sb[:], w2_raw[:], 4))
        nc.vector.tensor_copy(*woven(u16, u32, HALVES[0]))
        nc.vector.tensor_copy(*woven(u16, u32, slice(HALF, SPLIT)))
        nc.scalar.copy(*woven(u16, u32, slice(SPLIT, J)))
        for h in range(2):
            quantize_half(nc, uq, uqs, u16, h, E4M3)
        nc.scalar.copy(*dealt(w_sb[:].bitcast(U16), w_raw[:].bitcast(U16), 8))

        acc = [ps.tile([P, J], F32, name="acc%d" % t) for t in range(PACK)]
        for t in range(PACK):
            cols = slice(t * P, (t + 1) * P)
            nc.tensor.matmul_mx(
                out=acc[t][:], lhsT=w2_sb[:, cols].bitcast(E5M2), lhsT_scale=w2s_sb[:, cols],
                rhs=sx_sb[:].bitcast(E4M3), rhs_scale=sxs_sb, start=True, stop=False,
            )
        for t in range(PACK):
            cols = slice(t * P, (t + 1) * P)
            nc.tensor.matmul_mx(
                out=acc[t][:], lhsT=w_sb[:, 2 * t * P : 2 * (t + 1) * P].bitcast(E2M1), lhsT_scale=ws_sb[:, cols],
                rhs=uq[:].bitcast(E4M3), rhs_scale=uqs[:], start=False, stop=True,
            )

        tg = sb.tile([P, PACK, J], F32)
        pre = sb.tile([P, PACK, J], F32)
        last = PACK - 1
        for t in range(last):
            picked = tb_sb[t].indirect(offs2_sb[:])
            if t == 0:
                nc.vector.tensor_copy(tg[:, t, :], picked)
            else:
                nc.scalar.activation(tg[:, t, :], picked, COPY)
            nc.vector.tensor_tensor(pre[:, t, :], acc[t][:], tg[:, t, :], ALU.subtract)
        h16 = sb.tile([P, J, PACK], BF16, align_bytes=64)
        for h, half in enumerate(HALVES):
            nc.scalar.activation(tg[:, last, half], tb_sb[last].indirect(offs2_sb[:, 8 * h : 8 * h + 8]), COPY)
            nc.vector.tensor_tensor(pre[:, last, half], acc[last][:, half], tg[:, last, half], ALU.subtract)
        hq = sb.tile([P, J], U32, align_bytes=64)
        hqs = sb.tile([P, J], U8, align_bytes=64)
        for cols in (HALVES[0], slice(HALF, SPLIT)):
            dst, src = woven(h16, pre, cols)
            nc.vector.tensor_scalar(dst, src, 0.0, None, ALU.max)
        dst, src = woven(h16, pre, slice(SPLIT, J))
        nc.scalar.activation(dst, src, RELU)
        for h in range(2):
            quantize_half(nc, hq, hqs, h16, h, E5M2)

        out_rows = out.rearrange("(g p) j -> p g j", p=P)
        prod = [ps.tile([P, N // P, HALF], F32, name="prod%d" % h) for h in range(2)]
        y = [sb.tile([P, N // P, HALF], F32, name="y%d" % h) for h in range(2)]
        for h, half in enumerate(HALVES):
            for g in range(N // P):
                cols = slice(g * P, (g + 1) * P)
                nc.tensor.matmul_mx(
                    out=prod[h][:, g, :], lhsT=wb_sb[:, cols].bitcast(E5M2), lhsT_scale=wbs_sb[:, cols],
                    rhs=hq[:, half].bitcast(E5M2), rhs_scale=hqs[:, half], start=True, stop=True,
                )
        for h, half in enumerate(HALVES):
            nxt = slice(half.start + 1, min(half.stop + 1, J))
            nc.vector.scalar_tensor_tensor(
                rs_sb[:, :, nxt], prod[h][:, :, : nxt.stop - nxt.start], -1.4, rs_sb[:, :, nxt], ALU.mult, ALU.add
            )
        for h, half in enumerate(HALVES):
            nc.vector.scalar_tensor_tensor(y[h][:], rs_sb[:, :, half], 0.5, prod[h][:], ALU.mult, ALU.add)
            nc.sync.dma_start(out=out_rows[:, :, half], in_=y[h][:])
